import numpy as np
CORES = [3,11,19,27,35,43,51,59,131,259,387]
N = 11
ROOT = 3
WIDTHS = [256,25,128,128,256,256,128,128,25,128,25]
OFF = [0,256,281,409,537,793,1049,1177,1305,1330,1458]
C = 1483
def setup_inputs(rng):
    return {"x": rng.standard_normal((N, 128, C), dtype=np.float32)}
def reference(x):
    YW = max(WIDTHS)
    y = np.full((N, 128, YW), np.nan, x.dtype)
    for r in range(N):
        y[r][:, :WIDTHS[r]] = x[ROOT][:, OFF[r]:OFF[r] + WIDTHS[r]]
    return {"y": y}

@@ -1,0 +1,79 @@
+from concourse.bass import DstId, RemoteDMATransfer
+
+ROOT_RANK = 3
+
+SCRATCH = {
+    "b256": ("dram", [3, 128, 256], "float32"),
+    "b128": ("dram", [4, 128, 128], "float32"),
+    "b25": ("dram", [3, 128, 25], "float32"),
+}
+SLOT = {0: ("b256", 0), 4: ("b256", 1), 5: ("b256", 2),
+        9: ("b128", 0), 2: ("b128", 1), 6: ("b128", 2), 7: ("b128", 3),
+        1: ("b25", 0), 8: ("b25", 1), 10: ("b25", 2)}
+
+SEMAPHORES = ["ldA", "ldB", "ldC", "ldD", "own", "sent", "arr", "rel", "st"]
+
+LOADS = {
+    "sync": [(9, "ldA"), (0, "ldB"), (2, "ldC"), (7, "ldC"), (8, "ldD")],
+    "scalar": [(4, "ldB"), (5, "ldB"), (6, "ldC"), (1, "ldD"), (10, "ldD")],
+}
+CALLS = [
+    ("ldA", [(9, 131, 0, 8)]),
+    ("ldB", [(0, 30, 8, 4), (4, 31, 12, 4), (5, None, 0, 8)]),
+    ("ldC", [(2, None, 0, 4), (6, None, 4, 2), (7, None, 6, 2)]),
+    ("ldD", [(1, None, 0, 2), (8, None, 2, 2), (10, None, 4, 4)]),
+]
+
+
+def rank_program(g, core, T, topo):
+    W, OFF = T.tables["WIDTHS"], T.tables["OFF"]
+    cores = list(T.cores)
+    root = cores[ROOT_RANK]
+    rank = T.rank_of(core)
+
+    def slot(r):
+        name, k = SLOT[r]
+        return T[name][k]
+
+    forward = {}
+    arrive = {}
+    for _, trs in CALLS:
+        for r, via, lo, n in trs:
+            if via is None:
+                arrive[r] = n
+            else:
+                forward[via] = (r, n)
+                arrive[r] = 8
+
+    if core == root:
+        for qname, q in (("sync", g.sync), ("scalar", g.scalar)):
+            for r, s in LOADS[qname]:
+                q.dma_start(slot(r), T.x[:, OFF[r]:OFF[r] + W[r]]).then_inc(T.sem[s], 16)
+        g.sync.dma_start(T.y[:, 0:W[ROOT_RANK]], T.x[:, OFF[ROOT_RANK]:OFF[ROOT_RANK] + W[ROOT_RANK]]).then_inc(T.sem.own, 16)
+        sent = 0
+        for s, trs in CALLS:
+            g.wait_ge(T.sem[s], 16 * len(trs))
+            lst = []
+            for r, via, lo, n in trs:
+                dst = cores[r] if via is None else via
+                rid, pid = topo.addr(dst, core)
+                lst.append(RemoteDMATransfer(dst_ids=[DstId(rid=rid, pnc=pid)], dma_engine_mask=((1 << n) - 1) << lo,
+                                             remote_sem=T.sem.arr if via is None else T.sem.rel,
+                                             src=slot(r), dst=slot(r)))
+                sent += n
+            g.remote_dma_fused(lst, local_sem=T.sem.sent)
+        g.wait_ge(T.sem.sent, sent)
+        g.sync.wait_ge(T.sem.own, 16)
+        return
+
+    if core in forward:
+        r, n = forward[core]
+        rid, pid = topo.addr(cores[r], core)
+        g.wait_ge(T.sem.rel, n)
+        g.remote_dma(slot(r), slot(r), T.sem.arr, T.sem.sent, pid, rid, 0xFF)
+        g.wait_ge(T.sem.sent, 8)
+
+    if rank is not None:
+        g.sync.wait_ge(T.sem.arr, arrive[rank])
+        g.sync.dma_start(T.y[:, 0:W[rank]], slot(rank)).then_inc(T.sem.st, 16)
+        g.sync.wait_ge(T.sem.st, 16)

@@ -1,27 +1,27 @@
 from concourse.bass import DstId, RemoteDMATransfer
 
 ROOT_RANK = 3
-
 SCRATCH = {
     "b256": ("dram", [3, 128, 256], "float32"),
-    "b128": ("dram", [4, 128, 128], "float32"),
+    "b128": ("dram", [3, 128, 128], "float32"),
+    "b9": ("dram", [4, 128, 32], "float32"),
     "b25": ("dram", [3, 128, 25], "float32"),
 }
 SLOT = {0: ("b256", 0), 4: ("b256", 1), 5: ("b256", 2),
-        9: ("b128", 0), 2: ("b128", 1), 6: ("b128", 2), 7: ("b128", 3),
-        1: ("b25", 0), 8: ("b25", 1), 10: ("b25", 2)}
-
+        2: ("b128", 0), 6: ("b128", 1), 7: ("b128", 2),
+        1: ("b25", 0), 8: ("b25", 1), 10: ("b25", 2),
+        90: ("b9", 0), 91: ("b9", 1), 92: ("b9", 2), 93: ("b9", 3)}
+OWNER = {90: 9, 91: 9, 92: 9, 93: 9}
 SEMAPHORES = ["ldA", "ldB", "ldC", "ldD", "own", "sent", "arr", "rel", "st"]
-
 LOADS = {
     "sync": [(9, "ldA"), (0, "ldB"), (2, "ldC"), (7, "ldC"), (8, "ldD")],
     "scalar": [(4, "ldB"), (5, "ldB"), (6, "ldC"), (1, "ldD"), (10, "ldD")],
 }
 CALLS = [
-    ("ldA", [(9, 131, 0, 8)]),
-    ("ldB", [(0, 30, 8, 4), (4, 31, 12, 4), (5, None, 0, 8)]),
-    ("ldC", [(2, None, 0, 4), (6, None, 4, 2), (7, None, 6, 2)]),
-    ("ldD", [(1, None, 0, 2), (8, None, 2, 2), (10, None, 4, 4)]),
+    ("ldA", 1, [(90, 129, 0, 2), (91, 131, 2, 2), (92, 133, 4, 2), (93, 135, 6, 2)]),
+    ("ldB", 3, [(0, 30, 8, 4), (4, 31, 12, 4), (5, None, 0, 8)]),
+    ("ldC", 3, [(2, None, 0, 4), (6, None, 4, 2), (7, None, 6, 2)]),
+    ("ldD", 3, [(1, None, 0, 2), (8, None, 2, 2), (10, None, 4, 4)]),
 ]
 
 
@@ -31,19 +31,22 @@ def rank_program(g, core, T, topo):
     root = cores[ROOT_RANK]
     rank = T.rank_of(core)
 
-    def slot(r):
-        name, k = SLOT[r]
-        return T[name][k]
+    def slot(k):
+        if k == 9:
+            return T.b9[:]
+        name, i = SLOT[k]
+        return T[name][i]
 
     forward = {}
     arrive = {}
-    for _, trs in CALLS:
-        for r, via, lo, n in trs:
+    for _, _, trs in CALLS:
+        for k, via, lo, n in trs:
+            r = OWNER.get(k, k)
             if via is None:
-                arrive[r] = n
+                arrive[r] = arrive.get(r, 0) + n
             else:
-                forward[via] = (r, n)
-                arrive[r] = 8
+                forward[via] = (k, n)
+                arrive[r] = arrive.get(r, 0) + 8
 
     if core == root:
         for qname, q in (("sync", g.sync), ("scalar", g.scalar)):
@@ -51,15 +54,15 @@ def rank_program(g, core, T, topo):
                 q.dma_start(slot(r), T.x[:, OFF[r]:OFF[r] + W[r]]).then_inc(T.sem[s], 16)
         g.sync.dma_start(T.y[:, 0:W[ROOT_RANK]], T.x[:, OFF[ROOT_RANK]:OFF[ROOT_RANK] + W[ROOT_RANK]]).then_inc(T.sem.own, 16)
         sent = 0
-        for s, trs in CALLS:
-            g.wait_ge(T.sem[s], 16 * len(trs))
+        for s, nl, trs in CALLS:
+            g.wait_ge(T.sem[s], 16 * nl)
             lst = []
-            for r, via, lo, n in trs:
-                dst = cores[r] if via is None else via
+            for k, via, lo, n in trs:
+                dst = cores[k] if via is None else via
                 rid, pid = topo.addr(dst, core)
                 lst.append(RemoteDMATransfer(dst_ids=[DstId(rid=rid, pnc=pid)], dma_engine_mask=((1 << n) - 1) << lo,
                                              remote_sem=T.sem.arr if via is None else T.sem.rel,
-                                             src=slot(r), dst=slot(r)))
+                                             src=slot(k), dst=slot(k)))
                 sent += n
             g.remote_dma_fused(lst, local_sem=T.sem.sent)
         g.wait_ge(T.sem.sent, sent)
@@ -67,10 +70,10 @@ def rank_program(g, core, T, topo):
         return
 
     if core in forward:
-        r, n = forward[core]
-        rid, pid = topo.addr(cores[r], core)
+        k, n = forward[core]
+        rid, pid = topo.addr(cores[OWNER.get(k, k)], core)
         g.wait_ge(T.sem.rel, n)
-        g.remote_dma(slot(r), slot(r), T.sem.arr, T.sem.sent, pid, rid, 0xFF)
+        g.remote_dma(slot(k), slot(k), T.sem.arr, T.sem.sent, pid, rid, 0xFF)
         g.wait_ge(T.sem.sent, 8)
 
     if rank is not None:

@@ -19,7 +19,7 @@ LOADS = {
 }
 CALLS = [
     ("ldA", 1, [(90, 129, 0, 2), (91, 131, 2, 2), (92, 133, 4, 2), (93, 135, 6, 2)]),
-    ("ldB", 3, [(0, 30, 8, 4), (4, 31, 12, 4), (5, None, 0, 8)]),
+    ("ldB", 3, [(0, 30, 8, 8), (4, None, 0, 4), (5, None, 4, 4)]),
     ("ldC", 3, [(2, None, 0, 4), (6, None, 4, 2), (7, None, 6, 2)]),
     ("ldD", 3, [(1, None, 0, 2), (8, None, 2, 2), (10, None, 4, 4)]),
 ]

@@ -13,12 +13,10 @@ SLOT = {0: ("b256", 0), 4: ("b256", 1), 5: ("b256", 2),
         90: ("b9", 0), 91: ("b9", 1), 92: ("b9", 2), 93: ("b9", 3)}
 OWNER = {90: 9, 91: 9, 92: 9, 93: 9}
 SEMAPHORES = ["ldA", "ldB", "ldC", "ldD", "own", "sent", "arr", "rel", "st"]
-LOADS = {
-    "sync": [(9, "ldA"), (0, "ldB"), (2, "ldC"), (7, "ldC"), (8, "ldD")],
-    "scalar": [(4, "ldB"), (5, "ldB"), (6, "ldC"), (1, "ldD"), (10, "ldD")],
-}
+EARLY = {"sync": [(0, "ldB")], "scalar": [(4, "ldB"), (5, "ldB")]}
+LATE = {"sync": [(2, "ldC"), (6, "ldC"), (8, "ldD"), (10, "ldD")], "scalar": [(7, "ldC"), (1, "ldD")]}
 CALLS = [
-    ("ldA", 1, [(90, 129, 0, 2), (91, 131, 2, 2), (92, 133, 4, 2), (93, 135, 6, 2)]),
+    ("ldA", 2, [(90, 129, 0, 2), (91, 131, 2, 2), (92, 133, 4, 2), (93, 135, 6, 2)]),
     ("ldB", 3, [(0, 30, 8, 8), (4, None, 0, 4), (5, None, 4, 4)]),
     ("ldC", 3, [(2, None, 0, 4), (6, None, 4, 2), (7, None, 6, 2)]),
     ("ldD", 3, [(1, None, 0, 2), (8, None, 2, 2), (10, None, 4, 4)]),
@@ -49,10 +47,16 @@ def rank_program(g, core, T, topo):
                 arrive[r] = arrive.get(r, 0) + 8
 
     if core == root:
-        for qname, q in (("sync", g.sync), ("scalar", g.scalar)):
-            for r, s in LOADS[qname]:
+        qs = (("sync", g.sync), ("scalar", g.scalar))
+        for h, (qname, q) in enumerate(qs):
+            q.dma_start(T.b9[2 * h:2 * h + 2], T.x[64 * h:64 * h + 64, OFF[9]:OFF[9] + W[9]]).then_inc(T.sem.ldA, 16)
+            for r, s in EARLY[qname]:
                 q.dma_start(slot(r), T.x[:, OFF[r]:OFF[r] + W[r]]).then_inc(T.sem[s], 16)
-        g.sync.dma_start(T.y[:, 0:W[ROOT_RANK]], T.x[:, OFF[ROOT_RANK]:OFF[ROOT_RANK] + W[ROOT_RANK]]).then_inc(T.sem.own, 16)
+        for qname, q in qs:
+            q.wait_ge(T.sem.ldA, 32)
+            for r, s in LATE[qname]:
+                q.dma_start(slot(r), T.x[:, OFF[r]:OFF[r] + W[r]]).then_inc(T.sem[s], 16)
+        g.scalar.dma_start(T.y[:, 0:W[ROOT_RANK]], T.x[:, OFF[ROOT_RANK]:OFF[ROOT_RANK] + W[ROOT_RANK]]).then_inc(T.sem.own, 16)
         sent = 0
         for s, nl, trs in CALLS:
             g.wait_ge(T.sem[s], 16 * nl)
@@ -66,7 +70,7 @@ def rank_program(g, core, T, topo):
                 sent += n
             g.remote_dma_fused(lst, local_sem=T.sem.sent)
         g.wait_ge(T.sem.sent, sent)
-        g.sync.wait_ge(T.sem.own, 16)
+        g.scalar.wait_ge(T.sem.own, 16)
         return
 
     if core in forward:

from concourse.bass import DstId, RemoteDMATransfer

ROOT_RANK = 3
SCRATCH = {
    "b256": ("dram", [3, 128, 256], "float32"),
    "b128": ("dram", [3, 128, 128], "float32"),
    "b9": ("dram", [4, 128, 32], "float32"),
    "b25": ("dram", [3, 128, 25], "float32"),
}
SLOT = {0: ("b256", 0), 4: ("b256", 1), 5: ("b256", 2),
        2: ("b128", 0), 6: ("b128", 1), 7: ("b128", 2),
        1: ("b25", 0), 8: ("b25", 1), 10: ("b25", 2),
        90: ("b9", 0), 91: ("b9", 1), 92: ("b9", 2), 93: ("b9", 3)}
OWNER = {90: 9, 91: 9, 92: 9, 93: 9}
SEMAPHORES = ["ldA", "ldB", "ldC", "ldD", "own", "sent", "arr", "rel", "st"]
EARLY = {"sync": [(0, "ldB")], "scalar": [(4, "ldB"), (5, "ldB")]}
LATE = {"sync": [(2, "ldC"), (6, "ldC"), (8, "ldD"), (10, "ldD")], "scalar": [(7, "ldC"), (1, "ldD")]}
CALLS = [
    ("ldA", 2, [(90, 129, 0, 2), (91, 131, 2, 2), (92, 133, 4, 2), (93, 135, 6, 2)]),
    ("ldB", 3, [(0, 30, 8, 8), (4, None, 0, 4), (5, None, 4, 4)]),
    ("ldC", 3, [(2, None, 0, 4), (6, None, 4, 2), (7, None, 6, 2)]),
    ("ldD", 3, [(1, None, 0, 2), (8, None, 2, 2), (10, None, 4, 4)]),
]


def rank_program(g, core, T, topo):
    W, OFF = T.tables["WIDTHS"], T.tables["OFF"]
    cores = list(T.cores)
    root = cores[ROOT_RANK]
    rank = T.rank_of(core)

    def slot(k):
        if k == 9:
            return T.b9[:]
        name, i = SLOT[k]
        return T[name][i]

    forward = {}
    arrive = {}
    for _, _, trs in CALLS:
        for k, via, lo, n in trs:
            r = OWNER.get(k, k)
            if via is None:
                arrive[r] = arrive.get(r, 0) + n
            else:
                forward[via] = (k, n)
                arrive[r] = arrive.get(r, 0) + 8

    if core == root:
        qs = (("sync", g.sync), ("scalar", g.scalar))
        for h, (qname, q) in enumerate(qs):
            q.dma_start(T.b9[2 * h:2 * h + 2], T.x[64 * h:64 * h + 64, OFF[9]:OFF[9] + W[9]]).then_inc(T.sem.ldA, 16)
            for r, s in EARLY[qname]:
                q.dma_start(slot(r), T.x[:, OFF[r]:OFF[r] + W[r]]).then_inc(T.sem[s], 16)
        for qname, q in qs:
            q.wait_ge(T.sem.ldA, 32)
            for r, s in LATE[qname]:
                q.dma_start(slot(r), T.x[:, OFF[r]:OFF[r] + W[r]]).then_inc(T.sem[s], 16)
        g.scalar.dma_start(T.y[:, 0:W[ROOT_RANK]], T.x[:, OFF[ROOT_RANK]:OFF[ROOT_RANK] + W[ROOT_RANK]]).then_inc(T.sem.own, 16)
        sent = 0
        for s, nl, trs in CALLS:
            g.wait_ge(T.sem[s], 16 * nl)
            lst = []
            for k, via, lo, n in trs:
                dst = cores[k] if via is None else via
                rid, pid = topo.addr(dst, core)
                lst.append(RemoteDMATransfer(dst_ids=[DstId(rid=rid, pnc=pid)], dma_engine_mask=((1 << n) - 1) << lo,
                                             remote_sem=T.sem.arr if via is None else T.sem.rel,
                                             src=slot(k), dst=slot(k)))
                sent += n
            g.remote_dma_fused(lst, local_sem=T.sem.sent)
        g.wait_ge(T.sem.sent, sent)
        g.scalar.wait_ge(T.sem.own, 16)
        return

    if core in forward:
        k, n = forward[core]
        rid, pid = topo.addr(cores[OWNER.get(k, k)], core)
        g.wait_ge(T.sem.rel, n)
        g.remote_dma(slot(k), slot(k), T.sem.arr, T.sem.sent, pid, rid, 0xFF)
        g.wait_ge(T.sem.sent, 8)

    if rank is not None:
        g.sync.wait_ge(T.sem.arr, arrive[rank])
        g.sync.dma_start(T.y[:, 0:W[rank]], slot(rank)).then_inc(T.sem.st, 16)
        g.sync.wait_ge(T.sem.st, 16)
